import numpy as np, ml_dtypes
CORES = [2,42,66,74,82,90,114]
N = 7
KB, QP = 1, 256
WB = 3
def setup_inputs(rng):
    q = rng.standard_normal((N, 128, QP), dtype=np.float32) / 4; k = rng.standard_normal((N, 128, KB * 128), dtype=np.float32)
    a = 2 * np.pi * rng.random((N, QP)); s = 400 * rng.random((N, QP)) ** 1.5; q[:, 0, :] = s * np.cos(a); q[:, 1, :] = s * np.sin(a); q[:, 2, :] = 150 * rng.standard_normal((N, QP)); k[:, 2, :] = 1 + k[:, 2, :] / 50
    a = (2 * np.pi * rng.random() + np.pi / 2 * (rng.permutation(N).reshape(N, 1, 1) + 0.5) / N - 0.5 + (np.arange(KB).reshape(1, KB, 1) + rng.random((N, KB, 128))) / KB).reshape(N, KB * 128); k[:, 0, :] = np.cos(a); k[:, 1, :] = np.sin(a)
    return {"q": q.astype(ml_dtypes.bfloat16), "k": k.astype(ml_dtypes.bfloat16), "v": rng.standard_normal((N, 128, KB * 128), dtype=np.float32).astype(ml_dtypes.bfloat16)}
def setup_inputs_big(rng):
    d = setup_inputs(rng)
    for k in ("v",): d[k] = (d[k].astype(np.float32) * 1048576.0).astype(d[k].dtype)
    return d
def setup_inputs_small(rng):
    d = setup_inputs(rng)
    for k in ("v",): d[k] = (d[k].astype(np.float32) * (1 / 1048576.0)).astype(d[k].dtype)
    return d
def reference(q, k, v):
    Q, K, V = q.astype(np.float64), k.astype(np.float64), v.astype(np.float64)
    y = np.zeros((N, QP, 128))
    for r in range(N):
        js = list(range(max(0, r - WB), r + 1))
        S = np.concatenate([K[j].T @ Q[r] for j in js], axis=0)
        P = np.exp(S - S.max(axis=0)); P = P / P.sum(axis=0)
        y[r] = P.T @ np.concatenate([V[j][:, 128 * b:128 * b + 128] for j in js for b in range(KB)], axis=0)
    return {"y": y.astype(ml_dtypes.bfloat16)}

@@ -1,0 +1,185 @@
+from concourse.mybir import AluOpType, AxisListType, ActivationFunctionType
+
+NBMAX = 4
+WB = 3
+KVW = 264
+AW = 132
+
+SCRATCH = {
+    "kv": ("sbuf", [128, NBMAX * KVW], "bfloat16"),
+    "qs": ("sbuf", [128, 256], "bfloat16"),
+    "ones": ("sbuf", [128, 128], "bfloat16"),
+    "ident": ("sbuf", [128, 128], "bfloat16"),
+    "negm": ("sbuf", [128, 2 * NBMAX], "float32"),
+    "resc": ("sbuf", [128, 2 * NBMAX], "float32"),
+    "p": ("sbuf", [128, 2 * NBMAX * 128], "bfloat16"),
+    "pt": ("sbuf", [128, 2 * NBMAX * 128], "bfloat16"),
+    "tsc": ("sbuf", [128, 2 * NBMAX * AW], "float32"),
+    "acc": ("sbuf", [128, 2 * NBMAX * AW], "float32"),
+    "rcp": ("sbuf", [128, 2], "float32"),
+    "ysb": ("sbuf", [128, 256], "bfloat16"),
+    "st0": ("psum", [128, 512], "float32"),
+    "st1": ("psum", [128, 512], "float32"),
+    "tp0": ("psum", [128, 1024], "bfloat16"),
+    "tp1": ("psum", [128, 1024], "bfloat16"),
+    "o0": ("psum", [128, 512], "float32"),
+    "o1": ("psum", [128, 512], "float32"),
+}
+
+_STAGES = ["st", "rd", "ex", "wr", "tr", "cp", "pv", "aa", "tt", "ad"]
+SEMAPHORES = (["ldk", "ldv", "ldq", "m1", "mo", "idn", "sent", "rc", "sc0", "sc1", "yo0", "yo1"]
+              + ["arr%d" % b for b in range(1, NBMAX)]
+              + ["%s%d%d" % (s, b, i) for s in _STAGES for b in range(NBMAX) for i in range(2)])
+
+
+def _hops(topo, a, b):
+    ca, cb = topo.chip(a), topo.chip(b)
+    if ca == cb:
+        return 0
+    return 1 if (topo.mates(ca, cb) or topo.same_plane(ca, cb)) else 2
+
+
+def _distance_order(topo, cores):
+    n = len(cores)
+
+    def mean_hops(d):
+        h = [_hops(topo, cores[s], cores[s + d]) for s in range(n - d)]
+        return sum(h) / len(h)
+    return sorted(range(1, WB + 1), key=lambda d: -mean_hops(d))
+
+
+def rank_program(g, core, T, topo):
+    rank = T.rank_of(core)
+    if rank is None:
+        return
+    cores = list(T.cores)
+    n = len(cores)
+    dord = _distance_order(topo, cores)
+
+    def blocks(r):
+        return [r] + [r - d for d in dord if r - d >= 0]
+
+    mine = blocks(rank)
+    nb = len(mine)
+    last = nb - 1
+    dests = [rank + d for d in dord if rank + d < n]
+
+    def S(stage, b, i):
+        return T.sem["%s%d%d" % (stage, b, i)]
+
+    pe, dve, act, syn = g.tensor, g.vector, g.scalar, g.sync
+    Exp, Copy = ActivationFunctionType.Exp, ActivationFunctionType.Copy
+    st, tp, o = [T.st0, T.st1], [T.tp0, T.tp1], [T.o0, T.o1]
+
+    def kblk(b):
+        return T.kv[:, b * KVW:b * KVW + 128]
+
+    def vaug(b):
+        return T.kv[:, b * KVW + 128:b * KVW + 257]
+
+    def col(t, b, i):
+        return t[:, 2 * b + i:2 * b + i + 1]
+
+    def sq(t, b, i):
+        c = (2 * b + i) * 128
+        return t[:, c:c + 128]
+
+    def slot(t, b, i, w):
+        c = (2 * b + i) * AW
+        return t[:, c:c + w]
+
+    syn.dma_start(T.kv[:, 0:128], T.k[:]).then_inc(T.sem.ldk, 16)
+    act.dma_start(T.kv[:, 128:256], T.v[:]).then_inc(T.sem.ldv, 16)
+    syn.dma_start(T.qs[:], T.q[:]).then_inc(T.sem.ldq, 16)
+
+    dve.memset(T.ones[:], 1.0).then_inc(T.sem.m1, 1)
+    for b in range(nb):
+        dve.memset(T.kv[:, b * KVW + 256:b * KVW + 264], 1.0).then_inc(T.sem.mo, 1)
+    g.wait_ge(T.sem.m1, 1)
+    g.affine_select(T.ident[:], T.ones[:], [[-1, 128]], AluOpType.is_equal, 0.0, 0, 1).then_inc(T.sem.idn, 1)
+
+    sent = 0
+    if dests:
+        g.wait_ge(T.sem.ldk, 16)
+        g.wait_ge(T.sem.ldv, 16)
+    for dr in dests:
+        dst = cores[dr]
+        assert topo.may_write(core, dst)
+        rid, pid, _ = topo.addr(dst)
+        mask = topo.mask(core, dst)
+        b = blocks(dr).index(rank)
+        g.remote_dma(T.kv[:, b * KVW:b * KVW + 256], T.kv[:, 0:256], T.sem["arr%d" % b], T.sem.sent,
+                     pid, rid, mask)
+        sent += bin(mask).count("1")
+
+    for b in range(nb):
+        if b == 0:
+            pe.wait_ge(T.sem.ldk, 16)
+            pe.wait_ge(T.sem.ldq, 16)
+        else:
+            pe.wait_ge(T.sem["arr%d" % b], bin(topo.mask(cores[mine[b]], core)).count("1"))
+        for i in range(2):
+            if b > 0:
+                pe.wait_ge(S("wr", b - 1, i), 1)
+            pe.matmul(st[i][:, 0:128], T.qs[:, 128 * i:128 * i + 128], kblk(b), True, True).then_inc(S("st", b, i), 1)
+        for i in range(2):
+            dve.wait_ge(S("st", b, i), 1)
+            dve.tensor_reduce(col(T.negm, b, i), st[i][:, 0:(128 if b == 0 else 129)], AxisListType.X,
+                              AluOpType.max, negate=True).then_inc(S("rd", b, i), 1)
+        for i in range(2):
+            act.wait_ge(S("rd", b, i), 1)
+            act.activation(sq(T.p, b, i), st[i][:, 0:128], Exp, bias=col(T.negm, b, i)).then_inc(S("ex", b, i), 1)
+        for i in range(2):
+            pe.wait_ge(S("ex", b, i), 1)
+            if b == 0 and i == 0:
+                pe.wait_ge(T.sem.idn, 1)
+            pe.transpose(tp[i][:, 0:128], sq(T.p, b, i), T.ident[:]).then_inc(S("tr", b, i), 1)
+        for i in range(2):
+            dve.wait_ge(S("tr", b, i), 1)
+            dve.tensor_copy(sq(T.pt, b, i), tp[i][:, 0:128]).then_inc(S("cp", b, i), 1)
+        if b < last:
+            for i in range(2):
+                act.activation(st[i][:, 128:129], col(T.negm, b, i), Copy, scale=-1.0).then_inc(S("wr", b, i), 1)
+        if b > 0:
+            for i in range(2):
+                act.activation(col(T.resc, b, i), col(T.negm, b - 1, i), Exp, bias=col(T.negm, b, i),
+                               scale=-1.0).then_inc(S("aa", b, i), 1)
+            for i in range(2):
+                act.wait_ge(S("aa", b, i), 1)
+                act.wait_ge(S("ad", b - 1, i), 1)
+                act.activation(slot(T.tsc, b, i, 129), slot(T.acc, b - 1, i, 129), Copy,
+                               scale=col(T.resc, b, i)).then_inc(S("tt", b, i), 1)
+        for i in range(2):
+            pe.wait_ge(S("cp", b, i), 1)
+            if b == 0 and i == 0:
+                pe.wait_ge(T.sem.ldv, 16)
+                pe.wait_ge(T.sem.mo, nb)
+            if b > 0:
+                pe.wait_ge(S("ad", b - 1, i), 1)
+            pe.matmul(o[i][:, 0:129], sq(T.pt, b, i), vaug(b), True, True).then_inc(S("pv", b, i), 1)
+        for i in range(2):
+            dve.wait_ge(S("pv", b, i), 1)
+            if b == 0:
+                dve.tensor_copy(slot(T.acc, b, i, 129), o[i][:, 0:129]).then_inc(S("ad", b, i), 1)
+            else:
+                dve.wait_ge(S("tt", b, i), 1)
+                dve.tensor_tensor(slot(T.acc, b, i, 129), slot(T.tsc, b, i, 129), o[i][:, 0:129],
+                                  AluOpType.add).then_inc(S("ad", b, i), 1)
+
+    c0 = 2 * last * AW + 128
+    dve.wait_ge(S("ad", last, 0), 1)
+    dve.wait_ge(S("ad", last, 1), 1)
+    dve.reciprocal(T.rcp[:, 0:2], T.acc[:, c0:c0 + AW + 1:AW]).then_inc(T.sem.rc, 1)
+    act.wait_ge(T.sem.rc, 1)
+    act.activation(T.ysb[:, 0:128], slot(T.acc, last, 0, 128), Copy, scale=T.rcp[:, 0:1]).then_inc(T.sem.sc0, 1)
+    dve.wait_ge(T.sem.rc, 1)
+    dve.tensor_scalar(T.ysb[:, 128:256], slot(T.acc, last, 1, 128), T.rcp[:, 1:2], None,
+                      AluOpType.mult).then_inc(T.sem.sc1, 1)
+    act.wait_ge(T.sem.sc0, 1)
+    act.dma_start(T.y[0:128, :], T.ysb[:, 0:128]).then_inc(T.sem.yo0, 16)
+    syn.wait_ge(T.sem.sc1, 1)
+    syn.dma_start(T.y[128:256, :], T.ysb[:, 128:256]).then_inc(T.sem.yo1, 16)
+    act.wait_ge(T.sem.yo0, 16)
+    syn.wait_ge(T.sem.yo1, 16)
+    if sent:
+        g.wait_ge(T.sem.sent, sent)

@@ -1,3 +1,4 @@
+from concourse.bass import DstId, RemoteDMATransfer
 from concourse.mybir import AluOpType, AxisListType, ActivationFunctionType
 
 NBMAX = 4
@@ -12,6 +13,8 @@ SCRATCH = {
     "ident": ("sbuf", [128, 128], "bfloat16"),
     "negm": ("sbuf", [128, 2 * NBMAX], "float32"),
     "resc": ("sbuf", [128, 2 * NBMAX], "float32"),
+    "lsum": ("sbuf", [128, 2], "float32"),
+    "ltot": ("sbuf", [128, 2], "float32"),
     "p": ("sbuf", [128, 2 * NBMAX * 128], "bfloat16"),
     "pt": ("sbuf", [128, 2 * NBMAX * 128], "bfloat16"),
     "tsc": ("sbuf", [128, 2 * NBMAX * AW], "float32"),
@@ -27,8 +30,8 @@ SCRATCH = {
 }
 
 _STAGES = ["st", "rd", "ex", "wr", "tr", "cp", "pv", "aa", "tt", "ad"]
-SEMAPHORES = (["ldk", "ldv", "ldq", "m1", "mo", "idn", "sent", "rc", "sc0", "sc1", "yo0", "yo1"]
-              + ["arr%d" % b for b in range(1, NBMAX)]
+SEMAPHORES = (["ldk", "ldv", "ldq", "m1", "mo", "idn", "sent", "lt0", "lt1", "rc", "sc0", "sc1a", "sc1b", "yo0", "yo1"]
+              + ["ar%d" % m for m in range(NBMAX)]
               + ["%s%d%d" % (s, b, i) for s in _STAGES for b in range(NBMAX) for i in range(2)])
 
 
@@ -64,18 +67,20 @@ def rank_program(g, core, T, topo):
     last = nb - 1
     dests = [rank + d for d in dord if rank + d < n]
 
+    def sender_engines(sr):
+        m = -1
+        for d in dord:
+            if sr + d < n:
+                m &= topo.mask(cores[sr], cores[sr + d])
+        return bin(m).count("1")
+
     def S(stage, b, i):
         return T.sem["%s%d%d" % (stage, b, i)]
 
     pe, dve, act, syn = g.tensor, g.vector, g.scalar, g.sync
-    Exp, Copy = ActivationFunctionType.Exp, ActivationFunctionType.Copy
+    Exp, Copy, Ident = ActivationFunctionType.Exp, ActivationFunctionType.Copy, ActivationFunctionType.Identity
     st, tp, o = [T.st0, T.st1], [T.tp0, T.tp1], [T.o0, T.o1]
-
-    def kblk(b):
-        return T.kv[:, b * KVW:b * KVW + 128]
-
-    def vaug(b):
-        return T.kv[:, b * KVW + 128:b * KVW + 257]
+    LT = [T.sem.lt0, T.sem.lt1]
 
     def col(t, b, i):
         return t[:, 2 * b + i:2 * b + i + 1]
@@ -84,9 +89,12 @@ def rank_program(g, core, T, topo):
         c = (2 * b + i) * 128
         return t[:, c:c + 128]
 
-    def slot(t, b, i, w):
-        c = (2 * b + i) * AW
+    def slot(t, b, i, w, c0=0):
+        c = (2 * b + i) * AW + c0
         return t[:, c:c + w]
+
+    def width(b):
+        return 128 if b == last else 129
 
     syn.dma_start(T.kv[:, 0:128], T.k[:]).then_inc(T.sem.ldk, 16)
     act.dma_start(T.kv[:, 128:256], T.v[:]).then_inc(T.sem.ldv, 16)
@@ -102,53 +110,42 @@ def rank_program(g, core, T, topo):
     if dests:
         g.wait_ge(T.sem.ldk, 16)
         g.wait_ge(T.sem.ldv, 16)
-    for dr in dests:
-        dst = cores[dr]
-        assert topo.may_write(core, dst)
-        rid, pid, _ = topo.addr(dst)
-        mask = topo.mask(core, dst)
-        b = blocks(dr).index(rank)
-        g.remote_dma(T.kv[:, b * KVW:b * KVW + 256], T.kv[:, 0:256], T.sem["arr%d" % b], T.sem.sent,
-                     pid, rid, mask)
-        sent += bin(mask).count("1")
+        ids, outs = [], []
+        for dr in dests:
+            dst = cores[dr]
+            assert topo.may_write(core, dst)
+            rid, pid, _ = topo.addr(dst)
+            b = blocks(dr).index(rank)
+            ids.append(DstId(rid=rid, pnc=pid))
+            outs.append(T.kv[:, b * KVW:b * KVW + 256])
+        mask = topo.mask(core, cores[dests[0]])
+        for dr in dests:
+            mask &= topo.mask(core, cores[dr])
+        g.remote_dma_fused([RemoteDMATransfer(dst_ids=ids, dma_engine_mask=mask,
+                                              remote_sem=T.sem["ar%d" % (rank % NBMAX)],
+                                              srcs=[T.kv[:, 0:256]], dsts=outs, alu_op=0)], local_sem=T.sem.sent)
+        sent = bin(mask).count("1")
 
-    for b in range(nb):
+    def pe_scores(b):
         if b == 0:
             pe.wait_ge(T.sem.ldk, 16)
             pe.wait_ge(T.sem.ldq, 16)
         else:
-            pe.wait_ge(T.sem["arr%d" % b], bin(topo.mask(cores[mine[b]], core)).count("1"))
+            pe.wait_ge(T.sem["ar%d" % (mine[b] % NBMAX)], sender_engines(mine[b]))
         for i in range(2):
             if b > 0:
                 pe.wait_ge(S("wr", b - 1, i), 1)
-            pe.matmul(st[i][:, 0:128], T.qs[:, 128 * i:128 * i + 128], kblk(b), True, True).then_inc(S("st", b, i), 1)
-        for i in range(2):
-            dve.wait_ge(S("st", b, i), 1)
-            dve.tensor_reduce(col(T.negm, b, i), st[i][:, 0:(128 if b == 0 else 129)], AxisListType.X,
-                              AluOpType.max, negate=True).then_inc(S("rd", b, i), 1)
-        for i in range(2):
-            act.wait_ge(S("rd", b, i), 1)
-            act.activation(sq(T.p, b, i), st[i][:, 0:128], Exp, bias=col(T.negm, b, i)).then_inc(S("ex", b, i), 1)
+            pe.matmul(st[i][:, 0:128], T.qs[:, 128 * i:128 * i + 128], T.kv[:, b * KVW:b * KVW + 128],
+                      True, True).then_inc(S("st", b, i), 1)
+
+    def pe_transposes(b):
         for i in range(2):
             pe.wait_ge(S("ex", b, i), 1)
             if b == 0 and i == 0:
                 pe.wait_ge(T.sem.idn, 1)
             pe.transpose(tp[i][:, 0:128], sq(T.p, b, i), T.ident[:]).then_inc(S("tr", b, i), 1)
-        for i in range(2):
-            dve.wait_ge(S("tr", b, i), 1)
-            dve.tensor_copy(sq(T.pt, b, i), tp[i][:, 0:128]).then_inc(S("cp", b, i), 1)
-        if b < last:
-            for i in range(2):
-                act.activation(st[i][:, 128:129], col(T.negm, b, i), Copy, scale=-1.0).then_inc(S("wr", b, i), 1)
-        if b > 0:
-            for i in range(2):
-                act.activation(col(T.resc, b, i), col(T.negm, b - 1, i), Exp, bias=col(T.negm, b, i),
-                               scale=-1.0).then_inc(S("aa", b, i), 1)
-            for i in range(2):
-                act.wait_ge(S("aa", b, i), 1)
-                act.wait_ge(S("ad", b - 1, i), 1)
-                act.activation(slot(T.tsc, b, i, 129), slot(T.acc, b - 1, i, 129), Copy,
-                               scale=col(T.resc, b, i)).then_inc(S("tt", b, i), 1)
+
+    def pe_products(b):
         for i in range(2):
             pe.wait_ge(S("cp", b, i), 1)
             if b == 0 and i == 0:
@@ -156,29 +153,126 @@ def rank_program(g, core, T, topo):
                 pe.wait_ge(T.sem.mo, nb)
             if b > 0:
                 pe.wait_ge(S("ad", b - 1, i), 1)
-            pe.matmul(o[i][:, 0:129], sq(T.pt, b, i), vaug(b), True, True).then_inc(S("pv", b, i), 1)
+            pe.matmul(o[i][:, 0:width(b)], sq(T.pt, b, i), T.kv[:, b * KVW + 128:b * KVW + 128 + width(b)],
+                      True, True).then_inc(S("pv", b, i), 1)
+
+    def dve_max(b):
+        for i in range(2):
+            dve.wait_ge(S("st", b, i), 1)
+            dve.tensor_reduce(col(T.negm, b, i), st[i][:, 0:(128 if b == 0 else 129)], AxisListType.X,
+                              AluOpType.max, negate=True).then_inc(S("rd", b, i), 1)
+
+    def dve_copy(b, i):
+        dve.wait_ge(S("tr", b, i), 1)
+        dve.tensor_copy(sq(T.pt, b, i), tp[i][:, 0:128]).then_inc(S("cp", b, i), 1)
+
+    def act_copy(b, i):
+        act.wait_ge(S("tr", b, i), 1)
+        act.activation(sq(T.pt, b, i), tp[i][:, 0:128], Copy).then_inc(S("cp", b, i), 1)
+
+    def dve_fold(b):
+        w = width(b)
         for i in range(2):
             dve.wait_ge(S("pv", b, i), 1)
             if b == 0:
-                dve.tensor_copy(slot(T.acc, b, i, 129), o[i][:, 0:129]).then_inc(S("ad", b, i), 1)
+                dve.tensor_copy(slot(T.acc, b, i, w), o[i][:, 0:w]).then_inc(S("ad", b, i), 1)
             else:
                 dve.wait_ge(S("tt", b, i), 1)
-                dve.tensor_tensor(slot(T.acc, b, i, 129), slot(T.tsc, b, i, 129), o[i][:, 0:129],
+                dve.tensor_tensor(slot(T.acc, b, i, w), slot(T.tsc, b, i, w), o[i][:, 0:w],
                                   AluOpType.add).then_inc(S("ad", b, i), 1)
 
-    c0 = 2 * last * AW + 128
-    dve.wait_ge(S("ad", last, 0), 1)
-    dve.wait_ge(S("ad", last, 1), 1)
-    dve.reciprocal(T.rcp[:, 0:2], T.acc[:, c0:c0 + AW + 1:AW]).then_inc(T.sem.rc, 1)
+    def dve_reciprocal():
+        if last == 0:
+            dve.wait_ge(S("ex", 0, 0), 1)
+            dve.wait_ge(S("ex", 0, 1), 1)
+            den = T.lsum[:, 0:2]
+        else:
+            dve.wait_ge(LT[0], 1)
+            dve.wait_ge(LT[1], 1)
+            den = T.ltot[:, 0:2]
+        dve.reciprocal(T.rcp[:, 0:2], den).then_inc(T.sem.rc, 1)
+
+    def act_weights(b):
+        for i in range(2):
+            act.wait_ge(S("rd", b, i), 1)
+            act.activation(sq(T.p, b, i), st[i][:, 0:128], Exp, bias=col(T.negm, b, i),
+                           accum_out=(T.lsum[:, i:i + 1] if b == last else None)).then_inc(S("ex", b, i), 1)
+        if b < last:
+            for i in range(2):
+                act.activation(st[i][:, 128:129], col(T.negm, b, i), Copy, scale=-1.0).then_inc(S("wr", b, i), 1)
+        if b > 0:
+            for i in range(2):
+                act.activation(col(T.resc, b, i), col(T.negm, b - 1, i), Exp, bias=col(T.negm, b, i),
+                               scale=-1.0).then_inc(S("aa", b, i), 1)
+
+    def act_rescale(b, i):
+        act.wait_ge(S("aa", b, i), 1)
+        act.wait_ge(S("ad", b - 1, i), 1)
+        act.activation(slot(T.tsc, b, i, width(b)), slot(T.acc, b - 1, i, width(b)), Copy,
+                       scale=col(T.resc, b, i)).then_inc(S("tt", b, i), 1)
+
+    def act_denominator(i):
+        act.wait_ge(S("aa", last, i), 1)
+        act.wait_ge(S("ex", last, i), 1)
+        act.wait_ge(S("ad", last - 1, i), 1)
+        act.activation(T.ltot[:, i:i + 1], slot(T.acc, last - 1, i, 1, 128), Ident, bias=T.lsum[:, i:i + 1],
+                       scale=col(T.resc, last, i)).then_inc(LT[i], 1)
+
+    pe_scores(0)
+    pe_transposes(0)
+    pe_products(0)
+    if nb > 1:
+        pe_scores(1)
+    for b in range(1, nb):
+        pe_transposes(b)
+        if b < last:
+            pe_scores(b + 1)
+        pe_products(b)
+
+    dve_max(0)
+    dve_copy(0, 0)
+    dve_copy(0, 1)
+    if last == 0:
+        dve_reciprocal()
+    dve_fold(0)
+    if nb > 1:
+        dve_max(1)
+    for b in range(1, nb):
+        dve_copy(b, 0)
+        if b < last:
+            dve_copy(b, 1)
+            dve_max(b + 1)
+        else:
+            dve_reciprocal()
+        dve_fold(b)
+
+    for b in range(nb):
+        act_weights(b)
+        if 0 < b < last:
+            act_rescale(b, 0)
+            act_rescale(b, 1)
+        elif b == last and b > 0:
+            act_denominator(0)
+            act_denominator(1)
+            act_rescale(b, 0)
+            act_copy(b, 1)
+            act_rescale(b, 1)
+
     act.wait_ge(T.sem.rc, 1)
+    act.wait_ge(S("ad", last, 0), 1)
     act.activation(T.ysb[:, 0:128], slot(T.acc, last, 0, 128), Copy, scale=T.rcp[:, 0:1]).then_inc(T.sem.sc0, 1)
     dve.wait_ge(T.sem.rc, 1)
-    dve.tensor_scalar(T.ysb[:, 128:256], slot(T.acc, last, 1, 128), T.rcp[:, 1:2], None,
-                      AluOpType.mult).then_inc(T.sem.sc1, 1)
+    dve.wait_ge(S("ad", last, 1), 1)
+    dve.tensor_scalar(T.ysb[:, 128:192], slot(T.acc, last, 1, 64), T.rcp[:, 1:2], None,
+                      AluOpType.mult).then_inc(T.sem.sc1a, 1)
+    act.wait_ge(S("ad", last, 1), 1)
+    act.activation(T.ysb[:, 192:256], slot(T.acc, last, 1, 64, 64), Copy,
+                   scale=T.rcp[:, 1:2]).then_inc(T.sem.sc1b, 1)
+    syn.wait_ge(T.sem.sc1a, 1)
+    syn.wait_ge(T.sem.sc1b, 1)
+    syn.dma_start(T.y[128:256, :], T.ysb[:, 128:256]).then_inc(T.sem.yo1, 16)
     act.wait_ge(T.sem.sc0, 1)
     act.dma_start(T.y[0:128, :], T.ysb[:, 0:128]).then_inc(T.sem.yo0, 16)
-    syn.wait_ge(T.sem.sc1, 1)
-    syn.dma_start(T.y[128:256, :], T.ysb[:, 128:256]).then_inc(T.sem.yo1, 16)
     act.wait_ge(T.sem.yo0, 16)
     syn.wait_ge(T.sem.yo1, 16)
     if sent:

@@ -11,27 +11,31 @@ SCRATCH = {
     "qs": ("sbuf", [128, 256], "bfloat16"),
     "ones": ("sbuf", [128, 128], "bfloat16"),
     "ident": ("sbuf", [128, 128], "bfloat16"),
-    "negm": ("sbuf", [128, 2 * NBMAX], "float32"),
-    "resc": ("sbuf", [128, 2 * NBMAX], "float32"),
-    "lsum": ("sbuf", [128, 2], "float32"),
+    "negm": ("sbuf", [128, 4], "float32"),
+    "resc": ("sbuf", [128, 2], "float32"),
+    "lsum": ("sbuf", [128, 8], "float32"),
     "ltot": ("sbuf", [128, 2], "float32"),
     "p": ("sbuf", [128, 2 * NBMAX * 128], "bfloat16"),
     "pt": ("sbuf", [128, 2 * NBMAX * 128], "bfloat16"),
-    "tsc": ("sbuf", [128, 2 * NBMAX * AW], "float32"),
-    "acc": ("sbuf", [128, 2 * NBMAX * AW], "float32"),
+    "tbf": ("sbuf", [128, 256], "bfloat16"),
+    "acc": ("sbuf", [128, 2 * AW], "float32"),
     "rcp": ("sbuf", [128, 2], "float32"),
     "ysb": ("sbuf", [128, 256], "bfloat16"),
     "st0": ("psum", [128, 512], "float32"),
     "st1": ("psum", [128, 512], "float32"),
-    "tp0": ("psum", [128, 1024], "bfloat16"),
-    "tp1": ("psum", [128, 1024], "bfloat16"),
-    "o0": ("psum", [128, 512], "float32"),
-    "o1": ("psum", [128, 512], "float32"),
+    "u0": ("psum", [128, 512], "float32"),
+    "u1": ("psum", [128, 512], "float32"),
+    "u2": ("psum", [128, 512], "float32"),
+    "u3": ("psum", [128, 512], "float32"),
+    "u4": ("psum", [128, 512], "float32"),
+    "u5": ("psum", [128, 512], "float32"),
 }
 
-_STAGES = ["st", "rd", "ex", "wr", "tr", "cp", "pv", "aa", "tt", "ad"]
-SEMAPHORES = (["ldk", "ldv", "ldq", "m1", "mo", "idn", "sent", "lt0", "lt1", "rc", "sc0", "sc1a", "sc1b", "yo0", "yo1"]
-              + ["ar%d" % m for m in range(NBMAX)]
+_STAGES = ["st", "ex", "tr", "cp"]
+_HALF = ["rd0", "rdg", "wr", "pv", "ad", "aa", "la", "tt", "fo", "ls", "sc", "yo"]
+SEMAPHORES = (["ldk", "ldv", "ldq", "m1", "mo", "idn", "sent", "rc"]
+              + ["ar%d" % m for m in range(NBMAX)] + ["av%d" % m for m in range(NBMAX)]
+              + ["%s_%d" % (s, i) for s in _HALF for i in range(2)]
               + ["%s%d%d" % (s, b, i) for s in _STAGES for b in range(NBMAX) for i in range(2)])
 
 
@@ -63,8 +67,8 @@ def rank_program(g, core, T, topo):
         return [r] + [r - d for d in dord if r - d >= 0]
 
     mine = blocks(rank)
-    nb = len(mine)
-    last = nb - 1
+    nr = len(mine) - 1
+    R = range(1, nr + 1)
     dests = [rank + d for d in dord if rank + d < n]
 
     def sender_engines(sr):
@@ -77,203 +81,170 @@ def rank_program(g, core, T, topo):
     def S(stage, b, i):
         return T.sem["%s%d%d" % (stage, b, i)]
 
-    pe, dve, act, syn = g.tensor, g.vector, g.scalar, g.sync
-    Exp, Copy, Ident = ActivationFunctionType.Exp, ActivationFunctionType.Copy, ActivationFunctionType.Identity
-    st, tp, o = [T.st0, T.st1], [T.tp0, T.tp1], [T.o0, T.o1]
-    LT = [T.sem.lt0, T.sem.lt1]
+    def H(stage, i):
+        return T.sem["%s_%d" % (stage, i)]
 
-    def col(t, b, i):
-        return t[:, 2 * b + i:2 * b + i + 1]
+    pe, dve, act, syn = g.tensor, g.vector, g.scalar, g.sync
+    Exp, Copy = ActivationFunctionType.Exp, ActivationFunctionType.Copy
+    st = [T.st0, T.st1]
+    u = [T.u0, T.u1, T.u2, T.u3, T.u4, T.u5]
 
     def sq(t, b, i):
         c = (2 * b + i) * 128
         return t[:, c:c + 128]
 
-    def slot(t, b, i, w, c0=0):
-        c = (2 * b + i) * AW + c0
-        return t[:, c:c + w]
+    def kblk(b):
+        return T.kv[:, b * KVW:b * KVW + 128]
 
-    def width(b):
-        return 128 if b == last else 129
+    def vblk(b):
+        return T.kv[:, b * KVW + 128:b * KVW + 256]
+
+    def qhalf(i):
+        return T.qs[:, 128 * i:128 * i + 128]
+
+    def acc(i, c0, w):
+        return T.acc[:, i * AW + c0:i * AW + c0 + w]
+
+    def ubank(b, i):
+        return u[2 + i] if b == 0 else u[2 * (b - 1) + i]
 
     syn.dma_start(T.kv[:, 0:128], T.k[:]).then_inc(T.sem.ldk, 16)
     act.dma_start(T.kv[:, 128:256], T.v[:]).then_inc(T.sem.ldv, 16)
     syn.dma_start(T.qs[:], T.q[:]).then_inc(T.sem.ldq, 16)
 
     dve.memset(T.ones[:], 1.0).then_inc(T.sem.m1, 1)
-    for b in range(nb):
-        dve.memset(T.kv[:, b * KVW + 256:b * KVW + 264], 1.0).then_inc(T.sem.mo, 1)
+    dve.memset(T.kv[:, 256:264], 1.0).then_inc(T.sem.mo, 1)
     g.wait_ge(T.sem.m1, 1)
     g.affine_select(T.ident[:], T.ones[:], [[-1, 128]], AluOpType.is_equal, 0.0, 0, 1).then_inc(T.sem.idn, 1)
 
     sent = 0
     if dests:
-        g.wait_ge(T.sem.ldk, 16)
-        g.wait_ge(T.sem.ldv, 16)
-        ids, outs = [], []
+        ids, slots = [], []
+        mask = topo.mask(core, cores[dests[0]])
         for dr in dests:
             dst = cores[dr]
             assert topo.may_write(core, dst)
+            mask &= topo.mask(core, dst)
             rid, pid, _ = topo.addr(dst)
-            b = blocks(dr).index(rank)
             ids.append(DstId(rid=rid, pnc=pid))
-            outs.append(T.kv[:, b * KVW:b * KVW + 256])
-        mask = topo.mask(core, cores[dests[0]])
-        for dr in dests:
-            mask &= topo.mask(core, cores[dr])
-        g.remote_dma_fused([RemoteDMATransfer(dst_ids=ids, dma_engine_mask=mask,
-                                              remote_sem=T.sem["ar%d" % (rank % NBMAX)],
-                                              srcs=[T.kv[:, 0:256]], dsts=outs, alu_op=0)], local_sem=T.sem.sent)
-        sent = bin(mask).count("1")
+            slots.append(blocks(dr).index(rank))
+        for loaded, name, part in ((T.sem.ldk, "ar", kblk), (T.sem.ldv, "av", vblk)):
+            g.wait_ge(loaded, 16)
+            g.remote_dma_fused([RemoteDMATransfer(dst_ids=ids, dma_engine_mask=mask,
+                                                  remote_sem=T.sem["%s%d" % (name, rank % NBMAX)],
+                                                  srcs=[part(0)], dsts=[part(b) for b in slots], alu_op=0)],
+                               local_sem=T.sem.sent)
+            sent += bin(mask).count("1")
 
-    def pe_scores(b):
-        if b == 0:
-            pe.wait_ge(T.sem.ldk, 16)
-            pe.wait_ge(T.sem.ldq, 16)
-        else:
-            pe.wait_ge(T.sem["ar%d" % (mine[b] % NBMAX)], sender_engines(mine[b]))
-        for i in range(2):
-            if b > 0:
-                pe.wait_ge(S("wr", b - 1, i), 1)
-            pe.matmul(st[i][:, 0:128], T.qs[:, 128 * i:128 * i + 128], T.kv[:, b * KVW:b * KVW + 128],
-                      True, True).then_inc(S("st", b, i), 1)
-
-    def pe_transposes(b):
-        for i in range(2):
-            pe.wait_ge(S("ex", b, i), 1)
-            if b == 0 and i == 0:
-                pe.wait_ge(T.sem.idn, 1)
-            pe.transpose(tp[i][:, 0:128], sq(T.p, b, i), T.ident[:]).then_inc(S("tr", b, i), 1)
-
-    def pe_products(b):
-        for i in range(2):
-            pe.wait_ge(S("cp", b, i), 1)
-            if b == 0 and i == 0:
-                pe.wait_ge(T.sem.ldv, 16)
-                pe.wait_ge(T.sem.mo, nb)
-            if b > 0:
-                pe.wait_ge(S("ad", b - 1, i), 1)
-            pe.matmul(o[i][:, 0:width(b)], sq(T.pt, b, i), T.kv[:, b * KVW + 128:b * KVW + 128 + width(b)],
-                      True, True).then_inc(S("pv", b, i), 1)
-
-    def dve_max(b):
-        for i in range(2):
-            dve.wait_ge(S("st", b, i), 1)
-            dve.tensor_reduce(col(T.negm, b, i), st[i][:, 0:(128 if b == 0 else 129)], AxisListType.X,
-                              AluOpType.max, negate=True).then_inc(S("rd", b, i), 1)
+    def pe_transpose(b, i):
+        pe.wait_ge(S("ex", b, i), 1)
+        pe.matmul(ubank(b, i)[:, 0:128], sq(T.p, b, i), T.ident[:], True, True).then_inc(S("tr", b, i), 1)
 
     def dve_copy(b, i):
         dve.wait_ge(S("tr", b, i), 1)
-        dve.tensor_copy(sq(T.pt, b, i), tp[i][:, 0:128]).then_inc(S("cp", b, i), 1)
+        dve.tensor_copy(sq(T.pt, b, i), ubank(b, i)[:, 0:128]).then_inc(S("cp", b, i), 1)
 
-    def act_copy(b, i):
-        act.wait_ge(S("tr", b, i), 1)
-        act.activation(sq(T.pt, b, i), tp[i][:, 0:128], Copy).then_inc(S("cp", b, i), 1)
-
-    def dve_fold(b):
-        w = width(b)
+    pe.wait_ge(T.sem.ldk, 16)
+    pe.wait_ge(T.sem.ldq, 16)
+    for i in range(2):
+        pe.matmul(st[i][:, 0:128], qhalf(i), kblk(0), True, True).then_inc(S("st", 0, i), 1)
+    for i in range(2):
+        dve.wait_ge(S("st", 0, i), 1)
+        dve.tensor_reduce(T.negm[:, i:i + 1], st[i][:, 0:128], AxisListType.X, AluOpType.max,
+                          negate=True).then_inc(H("rd0", i), 1)
+    for i in range(2):
+        act.wait_ge(H("rd0", i), 1)
+        act.activation(sq(T.p, 0, i), st[i][:, 0:128], Exp, bias=T.negm[:, i:i + 1]).then_inc(S("ex", 0, i), 1)
+    if nr:
         for i in range(2):
-            dve.wait_ge(S("pv", b, i), 1)
-            if b == 0:
-                dve.tensor_copy(slot(T.acc, b, i, w), o[i][:, 0:w]).then_inc(S("ad", b, i), 1)
-            else:
-                dve.wait_ge(S("tt", b, i), 1)
-                dve.tensor_tensor(slot(T.acc, b, i, w), slot(T.tsc, b, i, w), o[i][:, 0:w],
-                                  AluOpType.add).then_inc(S("ad", b, i), 1)
+            act.activation(st[i][:, 128 * nr:128 * nr + 1], T.negm[:, i:i + 1], Copy,
+                           scale=-1.0).then_inc(H("wr", i), 1)
+    pe.wait_ge(T.sem.idn, 1)
+    for i in range(2):
+        pe_transpose(0, i)
+    for i in range(2):
+        dve_copy(0, i)
+    pe.wait_ge(T.sem.ldv, 16)
+    pe.wait_ge(T.sem.mo, 1)
+    for i in range(2):
+        pe.wait_ge(S("cp", 0, i), 1)
+        pe.matmul(u[i][:, 0:129], sq(T.pt, 0, i), T.kv[:, 128:257], True, True).then_inc(H("pv", i), 1)
+    for i in range(2):
+        dve.wait_ge(H("pv", i), 1)
+        dve.tensor_copy(acc(i, 0, 129), u[i][:, 0:129]).then_inc(H("ad", i), 1)
 
-    def dve_reciprocal():
-        if last == 0:
-            dve.wait_ge(S("ex", 0, 0), 1)
-            dve.wait_ge(S("ex", 0, 1), 1)
-            den = T.lsum[:, 0:2]
-        else:
-            dve.wait_ge(LT[0], 1)
-            dve.wait_ge(LT[1], 1)
-            den = T.ltot[:, 0:2]
-        dve.reciprocal(T.rcp[:, 0:2], den).then_inc(T.sem.rc, 1)
-
-    def act_weights(b):
+    if nr == 0:
+        dve.wait_ge(H("ad", 0), 1)
+        dve.wait_ge(H("ad", 1), 1)
+        dve.reciprocal(T.rcp[:, 0:2], T.acc[:, 128:128 + AW + 1:AW]).then_inc(T.sem.rc, 1)
+        src = [acc(0, 0, 128), acc(1, 0, 128)]
+        act.wait_ge(H("ad", 0), 1)
+    else:
+        for b in R:
+            pe.wait_ge(T.sem["ar%d" % (mine[b] % NBMAX)], sender_engines(mine[b]))
+            for i in range(2):
+                if b == 1:
+                    pe.wait_ge(H("wr", i), 1)
+                pe.matmul(st[i][:, 128 * (b - 1):128 * b], qhalf(i), kblk(b), True, True).then_inc(S("st", b, i), 1)
         for i in range(2):
-            act.wait_ge(S("rd", b, i), 1)
-            act.activation(sq(T.p, b, i), st[i][:, 0:128], Exp, bias=col(T.negm, b, i),
-                           accum_out=(T.lsum[:, i:i + 1] if b == last else None)).then_inc(S("ex", b, i), 1)
-        if b < last:
-            for i in range(2):
-                act.activation(st[i][:, 128:129], col(T.negm, b, i), Copy, scale=-1.0).then_inc(S("wr", b, i), 1)
-        if b > 0:
-            for i in range(2):
-                act.activation(col(T.resc, b, i), col(T.negm, b - 1, i), Exp, bias=col(T.negm, b, i),
-                               scale=-1.0).then_inc(S("aa", b, i), 1)
-
-    def act_rescale(b, i):
-        act.wait_ge(S("aa", b, i), 1)
-        act.wait_ge(S("ad", b - 1, i), 1)
-        act.activation(slot(T.tsc, b, i, width(b)), slot(T.acc, b - 1, i, width(b)), Copy,
-                       scale=col(T.resc, b, i)).then_inc(S("tt", b, i), 1)
-
-    def act_denominator(i):
-        act.wait_ge(S("aa", last, i), 1)
-        act.wait_ge(S("ex", last, i), 1)
-        act.wait_ge(S("ad", last - 1, i), 1)
-        act.activation(T.ltot[:, i:i + 1], slot(T.acc, last - 1, i, 1, 128), Ident, bias=T.lsum[:, i:i + 1],
-                       scale=col(T.resc, last, i)).then_inc(LT[i], 1)
-
-    pe_scores(0)
-    pe_transposes(0)
-    pe_products(0)
-    if nb > 1:
-        pe_scores(1)
-    for b in range(1, nb):
-        pe_transposes(b)
-        if b < last:
-            pe_scores(b + 1)
-        pe_products(b)
-
-    dve_max(0)
-    dve_copy(0, 0)
-    dve_copy(0, 1)
-    if last == 0:
-        dve_reciprocal()
-    dve_fold(0)
-    if nb > 1:
-        dve_max(1)
-    for b in range(1, nb):
-        dve_copy(b, 0)
-        if b < last:
-            dve_copy(b, 1)
-            dve_max(b + 1)
-        else:
-            dve_reciprocal()
-        dve_fold(b)
-
-    for b in range(nb):
-        act_weights(b)
-        if 0 < b < last:
-            act_rescale(b, 0)
-            act_rescale(b, 1)
-        elif b == last and b > 0:
-            act_denominator(0)
-            act_denominator(1)
-            act_rescale(b, 0)
-            act_copy(b, 1)
-            act_rescale(b, 1)
+            for b in R:
+                dve.wait_ge(S("st", b, i), 1)
+            dve.tensor_reduce(T.negm[:, 2 + i:3 + i], st[i][:, 0:128 * nr + 1], AxisListType.X, AluOpType.max,
+                              negate=True).then_inc(H("rdg", i), 1)
+        for i in range(2):
+            act.wait_ge(H("rdg", i), 1)
+            for b in R:
+                act.activation(sq(T.p, b, i), st[i][:, 128 * (b - 1):128 * b], Exp, bias=T.negm[:, 2 + i:3 + i],
+                               accum_out=T.lsum[:, 4 * i + b - 1:4 * i + b]).then_inc(S("ex", b, i), 1)
+            act.activation(T.resc[:, i:i + 1], T.negm[:, i:i + 1], Exp, bias=T.negm[:, 2 + i:3 + i],
+                           scale=-1.0).then_inc(H("aa", i), 1)
+        for i in range(2):
+            act.wait_ge(H("aa", i), 1)
+            act.wait_ge(H("ad", i), 1)
+            act.activation(T.lsum[:, 4 * i + nr:4 * i + nr + 1], acc(i, 128, 1), Copy,
+                           scale=T.resc[:, i:i + 1]).then_inc(H("la", i), 1)
+        for i in range(2):
+            act.activation(T.tbf[:, 128 * i:128 * i + 128], acc(i, 0, 128), Copy,
+                           scale=T.resc[:, i:i + 1]).then_inc(H("tt", i), 1)
+        pe.wait_ge(H("ad", 0), 1)
+        pe.wait_ge(H("ad", 1), 1)
+        for i in range(2):
+            for b in R:
+                pe_transpose(b, i)
+        for i in range(2):
+            for b in R:
+                dve_copy(b, i)
+        for i in range(2):
+            for b in R:
+                pe.wait_ge(S("cp", b, i), 1)
+                if i == 0:
+                    pe.wait_ge(T.sem["av%d" % (mine[b] % NBMAX)], sender_engines(mine[b]))
+                pe.matmul(st[i][:, 0:128], sq(T.pt, b, i), vblk(b), b == 1, False)
+            pe.wait_ge(H("tt", i), 1)
+            pe.matmul(st[i][:, 0:128], T.ident[:], T.tbf[:, 128 * i:128 * i + 128], False,
+                      True).then_inc(H("fo", i), 1)
+        for i in range(2):
+            for b in R:
+                dve.wait_ge(S("ex", b, i), 1)
+            dve.wait_ge(H("la", i), 1)
+            dve.tensor_reduce(T.ltot[:, i:i + 1], T.lsum[:, 4 * i:4 * i + nr + 1], AxisListType.X,
+                              AluOpType.add).then_inc(H("ls", i), 1)
+        dve.wait_ge(H("ls", 0), 1)
+        dve.wait_ge(H("ls", 1), 1)
+        dve.reciprocal(T.rcp[:, 0:2], T.ltot[:, 0:2]).then_inc(T.sem.rc, 1)
+        src = [st[0][:, 0:128], st[1][:, 0:128]]
+        act.wait_ge(H("fo", 0), 1)
+        dve.wait_ge(H("fo", 1), 1)
 
     act.wait_ge(T.sem.rc, 1)
-    act.wait_ge(S("ad", last, 0), 1)
-    act.activation(T.ysb[:, 0:128], slot(T.acc, last, 0, 128), Copy, scale=T.rcp[:, 0:1]).then_inc(T.sem.sc0, 1)
+    act.activation(T.ysb[:, 0:128], src[0], Copy, scale=T.rcp[:, 0:1]).then_inc(H("sc", 0), 1)
     dve.wait_ge(T.sem.rc, 1)
-    dve.wait_ge(S("ad", last, 1), 1)
-    dve.tensor_scalar(T.ysb[:, 128:192], slot(T.acc, last, 1, 64), T.rcp[:, 1:2], None,
-                      AluOpType.mult).then_inc(T.sem.sc1a, 1)
-    act.wait_ge(S("ad", last, 1), 1)
-    act.activation(T.ysb[:, 192:256], slot(T.acc, last, 1, 64, 64), Copy,
-                   scale=T.rcp[:, 1:2]).then_inc(T.sem.sc1b, 1)
-    syn.wait_ge(T.sem.sc1a, 1)
-    syn.wait_ge(T.sem.sc1b, 1)
-    syn.dma_start(T.y[128:256, :], T.ysb[:, 128:256]).then_inc(T.sem.yo1, 16)
-    act.wait_ge(T.sem.sc0, 1)
-    act.dma_start(T.y[0:128, :], T.ysb[:, 0:128]).then_inc(T.sem.yo0, 16)
-    act.wait_ge(T.sem.yo0, 16)
-    syn.wait_ge(T.sem.yo1, 16)
+    dve.tensor_scalar(T.ysb[:, 128:256], src[1], T.rcp[:, 1:2], None, AluOpType.mult).then_inc(H("sc", 1), 1)
+    act.wait_ge(H("sc", 0), 1)
+    act.dma_start(T.y[0:128, :], T.ysb[:, 0:128]).then_inc(H("yo", 0), 16)
+    syn.wait_ge(H("sc", 1), 1)
+    syn.dma_start(T.y[128:256, :], T.ysb[:, 128:256]).then_inc(H("yo", 1), 16)
+    act.wait_ge(H("yo", 0), 16)
+    syn.wait_ge(H("yo", 1), 16)
     if sent:
         g.wait_ge(T.sem.sent, sent)

from concourse.bass import DstId, RemoteDMATransfer
from concourse.mybir import AluOpType, AxisListType, ActivationFunctionType

NBMAX = 4
WB = 3
KVW = 264
AW = 132

SCRATCH = {
    "kv": ("sbuf", [128, NBMAX * KVW], "bfloat16"),
    "qs": ("sbuf", [128, 256], "bfloat16"),
    "ones": ("sbuf", [128, 128], "bfloat16"),
    "ident": ("sbuf", [128, 128], "bfloat16"),
    "negm": ("sbuf", [128, 4], "float32"),
    "resc": ("sbuf", [128, 2], "float32"),
    "lsum": ("sbuf", [128, 8], "float32"),
    "ltot": ("sbuf", [128, 2], "float32"),
    "p": ("sbuf", [128, 2 * NBMAX * 128], "bfloat16"),
    "pt": ("sbuf", [128, 2 * NBMAX * 128], "bfloat16"),
    "tbf": ("sbuf", [128, 256], "bfloat16"),
    "acc": ("sbuf", [128, 2 * AW], "float32"),
    "rcp": ("sbuf", [128, 2], "float32"),
    "ysb": ("sbuf", [128, 256], "bfloat16"),
    "st0": ("psum", [128, 512], "float32"),
    "st1": ("psum", [128, 512], "float32"),
    "u0": ("psum", [128, 512], "float32"),
    "u1": ("psum", [128, 512], "float32"),
    "u2": ("psum", [128, 512], "float32"),
    "u3": ("psum", [128, 512], "float32"),
    "u4": ("psum", [128, 512], "float32"),
    "u5": ("psum", [128, 512], "float32"),
}

_STAGES = ["st", "ex", "tr", "cp"]
_HALF = ["rd0", "rdg", "wr", "pv", "ad", "aa", "la", "tt", "fo", "ls", "sc", "yo"]
SEMAPHORES = (["ldk", "ldv", "ldq", "m1", "mo", "idn", "sent", "rc"]
              + ["ar%d" % m for m in range(NBMAX)] + ["av%d" % m for m in range(NBMAX)]
              + ["%s_%d" % (s, i) for s in _HALF for i in range(2)]
              + ["%s%d%d" % (s, b, i) for s in _STAGES for b in range(NBMAX) for i in range(2)])


def _hops(topo, a, b):
    ca, cb = topo.chip(a), topo.chip(b)
    if ca == cb:
        return 0
    return 1 if (topo.mates(ca, cb) or topo.same_plane(ca, cb)) else 2


def _distance_order(topo, cores):
    n = len(cores)

    def mean_hops(d):
        h = [_hops(topo, cores[s], cores[s + d]) for s in range(n - d)]
        return sum(h) / len(h)
    return sorted(range(1, WB + 1), key=lambda d: -mean_hops(d))


def rank_program(g, core, T, topo):
    rank = T.rank_of(core)
    if rank is None:
        return
    cores = list(T.cores)
    n = len(cores)
    dord = _distance_order(topo, cores)

    def blocks(r):
        return [r] + [r - d for d in dord if r - d >= 0]

    mine = blocks(rank)
    nr = len(mine) - 1
    R = range(1, nr + 1)
    dests = [rank + d for d in dord if rank + d < n]

    def sender_engines(sr):
        m = -1
        for d in dord:
            if sr + d < n:
                m &= topo.mask(cores[sr], cores[sr + d])
        return bin(m).count("1")

    def S(stage, b, i):
        return T.sem["%s%d%d" % (stage, b, i)]

    def H(stage, i):
        return T.sem["%s_%d" % (stage, i)]

    pe, dve, act, syn = g.tensor, g.vector, g.scalar, g.sync
    Exp, Copy = ActivationFunctionType.Exp, ActivationFunctionType.Copy
    st = [T.st0, T.st1]
    u = [T.u0, T.u1, T.u2, T.u3, T.u4, T.u5]

    def sq(t, b, i):
        c = (2 * b + i) * 128
        return t[:, c:c + 128]

    def kblk(b):
        return T.kv[:, b * KVW:b * KVW + 128]

    def vblk(b):
        return T.kv[:, b * KVW + 128:b * KVW + 256]

    def qhalf(i):
        return T.qs[:, 128 * i:128 * i + 128]

    def acc(i, c0, w):
        return T.acc[:, i * AW + c0:i * AW + c0 + w]

    def ubank(b, i):
        return u[2 + i] if b == 0 else u[2 * (b - 1) + i]

    syn.dma_start(T.kv[:, 0:128], T.k[:]).then_inc(T.sem.ldk, 16)
    act.dma_start(T.kv[:, 128:256], T.v[:]).then_inc(T.sem.ldv, 16)
    syn.dma_start(T.qs[:], T.q[:]).then_inc(T.sem.ldq, 16)

    dve.memset(T.ones[:], 1.0).then_inc(T.sem.m1, 1)
    dve.memset(T.kv[:, 256:264], 1.0).then_inc(T.sem.mo, 1)
    g.wait_ge(T.sem.m1, 1)
    g.affine_select(T.ident[:], T.ones[:], [[-1, 128]], AluOpType.is_equal, 0.0, 0, 1).then_inc(T.sem.idn, 1)

    sent = 0
    if dests:
        ids, slots = [], []
        mask = topo.mask(core, cores[dests[0]])
        for dr in dests:
            dst = cores[dr]
            assert topo.may_write(core, dst)
            mask &= topo.mask(core, dst)
            rid, pid, _ = topo.addr(dst)
            ids.append(DstId(rid=rid, pnc=pid))
            slots.append(blocks(dr).index(rank))
        for loaded, name, part in ((T.sem.ldk, "ar", kblk), (T.sem.ldv, "av", vblk)):
            g.wait_ge(loaded, 16)
            g.remote_dma_fused([RemoteDMATransfer(dst_ids=ids, dma_engine_mask=mask,
                                                  remote_sem=T.sem["%s%d" % (name, rank % NBMAX)],
                                                  srcs=[part(0)], dsts=[part(b) for b in slots], alu_op=0)],
                               local_sem=T.sem.sent)
            sent += bin(mask).count("1")

    def pe_transpose(b, i):
        pe.wait_ge(S("ex", b, i), 1)
        pe.matmul(ubank(b, i)[:, 0:128], sq(T.p, b, i), T.ident[:], True, True).then_inc(S("tr", b, i), 1)

    def dve_copy(b, i):
        dve.wait_ge(S("tr", b, i), 1)
        dve.tensor_copy(sq(T.pt, b, i), ubank(b, i)[:, 0:128]).then_inc(S("cp", b, i), 1)

    pe.wait_ge(T.sem.ldk, 16)
    pe.wait_ge(T.sem.ldq, 16)
    for i in range(2):
        pe.matmul(st[i][:, 0:128], qhalf(i), kblk(0), True, True).then_inc(S("st", 0, i), 1)
    for i in range(2):
        dve.wait_ge(S("st", 0, i), 1)
        dve.tensor_reduce(T.negm[:, i:i + 1], st[i][:, 0:128], AxisListType.X, AluOpType.max,
                          negate=True).then_inc(H("rd0", i), 1)
    for i in range(2):
        act.wait_ge(H("rd0", i), 1)
        act.activation(sq(T.p, 0, i), st[i][:, 0:128], Exp, bias=T.negm[:, i:i + 1]).then_inc(S("ex", 0, i), 1)
    if nr:
        for i in range(2):
            act.activation(st[i][:, 128 * nr:128 * nr + 1], T.negm[:, i:i + 1], Copy,
                           scale=-1.0).then_inc(H("wr", i), 1)
    pe.wait_ge(T.sem.idn, 1)
    for i in range(2):
        pe_transpose(0, i)
    for i in range(2):
        dve_copy(0, i)
    pe.wait_ge(T.sem.ldv, 16)
    pe.wait_ge(T.sem.mo, 1)
    for i in range(2):
        pe.wait_ge(S("cp", 0, i), 1)
        pe.matmul(u[i][:, 0:129], sq(T.pt, 0, i), T.kv[:, 128:257], True, True).then_inc(H("pv", i), 1)
    for i in range(2):
        dve.wait_ge(H("pv", i), 1)
        dve.tensor_copy(acc(i, 0, 129), u[i][:, 0:129]).then_inc(H("ad", i), 1)

    if nr == 0:
        dve.wait_ge(H("ad", 0), 1)
        dve.wait_ge(H("ad", 1), 1)
        dve.reciprocal(T.rcp[:, 0:2], T.acc[:, 128:128 + AW + 1:AW]).then_inc(T.sem.rc, 1)
        src = [acc(0, 0, 128), acc(1, 0, 128)]
        act.wait_ge(H("ad", 0), 1)
    else:
        for b in R:
            pe.wait_ge(T.sem["ar%d" % (mine[b] % NBMAX)], sender_engines(mine[b]))
            for i in range(2):
                if b == 1:
                    pe.wait_ge(H("wr", i), 1)
                pe.matmul(st[i][:, 128 * (b - 1):128 * b], qhalf(i), kblk(b), True, True).then_inc(S("st", b, i), 1)
        for i in range(2):
            for b in R:
                dve.wait_ge(S("st", b, i), 1)
            dve.tensor_reduce(T.negm[:, 2 + i:3 + i], st[i][:, 0:128 * nr + 1], AxisListType.X, AluOpType.max,
                              negate=True).then_inc(H("rdg", i), 1)
        for i in range(2):
            act.wait_ge(H("rdg", i), 1)
            for b in R:
                act.activation(sq(T.p, b, i), st[i][:, 128 * (b - 1):128 * b], Exp, bias=T.negm[:, 2 + i:3 + i],
                               accum_out=T.lsum[:, 4 * i + b - 1:4 * i + b]).then_inc(S("ex", b, i), 1)
            act.activation(T.resc[:, i:i + 1], T.negm[:, i:i + 1], Exp, bias=T.negm[:, 2 + i:3 + i],
                           scale=-1.0).then_inc(H("aa", i), 1)
        for i in range(2):
            act.wait_ge(H("aa", i), 1)
            act.wait_ge(H("ad", i), 1)
            act.activation(T.lsum[:, 4 * i + nr:4 * i + nr + 1], acc(i, 128, 1), Copy,
                           scale=T.resc[:, i:i + 1]).then_inc(H("la", i), 1)
        for i in range(2):
            act.activation(T.tbf[:, 128 * i:128 * i + 128], acc(i, 0, 128), Copy,
                           scale=T.resc[:, i:i + 1]).then_inc(H("tt", i), 1)
        pe.wait_ge(H("ad", 0), 1)
        pe.wait_ge(H("ad", 1), 1)
        for i in range(2):
            for b in R:
                pe_transpose(b, i)
        for i in range(2):
            for b in R:
                dve_copy(b, i)
        for i in range(2):
            for b in R:
                pe.wait_ge(S("cp", b, i), 1)
                if i == 0:
                    pe.wait_ge(T.sem["av%d" % (mine[b] % NBMAX)], sender_engines(mine[b]))
                pe.matmul(st[i][:, 0:128], sq(T.pt, b, i), vblk(b), b == 1, False)
            pe.wait_ge(H("tt", i), 1)
            pe.matmul(st[i][:, 0:128], T.ident[:], T.tbf[:, 128 * i:128 * i + 128], False,
                      True).then_inc(H("fo", i), 1)
        for i in range(2):
            for b in R:
                dve.wait_ge(S("ex", b, i), 1)
            dve.wait_ge(H("la", i), 1)
            dve.tensor_reduce(T.ltot[:, i:i + 1], T.lsum[:, 4 * i:4 * i + nr + 1], AxisListType.X,
                              AluOpType.add).then_inc(H("ls", i), 1)
        dve.wait_ge(H("ls", 0), 1)
        dve.wait_ge(H("ls", 1), 1)
        dve.reciprocal(T.rcp[:, 0:2], T.ltot[:, 0:2]).then_inc(T.sem.rc, 1)
        src = [st[0][:, 0:128], st[1][:, 0:128]]
        act.wait_ge(H("fo", 0), 1)
        dve.wait_ge(H("fo", 1), 1)

    act.wait_ge(T.sem.rc, 1)
    act.activation(T.ysb[:, 0:128], src[0], Copy, scale=T.rcp[:, 0:1]).then_inc(H("sc", 0), 1)
    dve.wait_ge(T.sem.rc, 1)
    dve.tensor_scalar(T.ysb[:, 128:256], src[1], T.rcp[:, 1:2], None, AluOpType.mult).then_inc(H("sc", 1), 1)
    act.wait_ge(H("sc", 0), 1)
    act.dma_start(T.y[0:128, :], T.ysb[:, 0:128]).then_inc(H("yo", 0), 16)
    syn.wait_ge(H("sc", 1), 1)
    syn.dma_start(T.y[128:256, :], T.ysb[:, 128:256]).then_inc(H("yo", 1), 16)
    act.wait_ge(H("yo", 0), 16)
    syn.wait_ge(H("yo", 1), 16)
    if sent:
        g.wait_ge(T.sem.sent, sent)
